import numpy as np
import ml_dtypes


def mxq(x, axis, fmt="e4m3"):
    dtype, down = {"e4m3": (ml_dtypes.float8_e4m3fn, 7), "e5m2": (ml_dtypes.float8_e5m2, 14)}[fmt]
    v = np.moveaxis(np.asarray(x, np.float32).astype(ml_dtypes.bfloat16).astype(np.float64), axis, -1)
    blocks = v.reshape(v.shape[:-1] + (-1, 32))
    amax = np.abs(blocks).max(-1, keepdims=True)
    byte = np.maximum(np.where(amax > 0, np.frexp(amax)[1] - 1 + 127, 0) - down, 1)
    scale = np.exp2(byte - 127.0)
    codes = (blocks / scale).astype(np.float32).astype(dtype).astype(np.float64)
    return np.moveaxis((codes * scale).reshape(v.shape), -1, axis)


WIDE = False


def mx_kscale(k):
    if not WIDE:
        return np.ones(k)
    levels = np.array([10, -10, 5, -5, 0])
    if k % 512:
        return np.exp2(np.random.permutation(np.resize(levels, k // 32))).repeat(32)
    a = np.empty((k // 512, 16))
    for p in range(k // 512):
        a[p, :8] = np.random.permutation(np.resize(levels, 8))
        for g in range(8):
            far = levels[np.abs(levels - a[p, g]) >= 10]
            a[p, g + 8] = far[np.random.randint(len(far))]
    return np.exp2(a.ravel()).repeat(32)


def f64(x):
    return np.asarray(x).astype(np.float64)


def striped8(idx):
    return np.asarray(idx).reshape(8, -1, 16).transpose(0, 2, 1).reshape(128, -1).astype(np.uint16)


def unstriped8(offs):
    return offs.reshape(8, 16, -1).transpose(0, 2, 1).reshape(8, -1).astype(np.int64)


def pick8(x, idx, run):
    r = np.arange(len(x))
    return x[r[:, None], idx[r % (8 * run) // run]]


E2M1 = np.array([0.0, 0.5, 1.0, 1.5, 2.0, 3.0, 4.0, 6.0, -0.0, -0.5, -1.0, -1.5, -2.0, -3.0, -4.0, -6.0])


def pack_weight(w, fmt):
    k, n = w.shape
    w = f64(np.asarray(w, np.float32).astype(ml_dtypes.bfloat16)).reshape(k // 32, 32, n)
    amax = np.abs(w).max(1)
    if fmt == "e4m3":
        byte = np.frexp(amax)[1] - 1 + 127 - 7
    else:
        mant, ex = np.frexp(amax / 6.0)
        byte = np.where(mant > 0.5, ex, ex - 1) + 127
    byte = np.clip(np.where(amax > 0, byte, 1), 1, 254)
    scaled = (w * np.exp2(127.0 - byte)[:, None, :]).reshape(k, n).astype(np.float32)
    by_word = np.ascontiguousarray(scaled.reshape(k // 512, 128, 4, n).transpose(0, 1, 3, 2))
    if fmt == "e4m3":
        words = by_word.astype(ml_dtypes.float8_e4m3fn).view(np.uint8)
    else:
        c = by_word.astype(ml_dtypes.float4_e2m1fn).view(np.uint8) & 0xF
        words = (c[..., 0::2] | (c[..., 1::2] << 4)).reshape(k // 512, 128, 2 * n)
    return np.ascontiguousarray(words), np.ascontiguousarray(byte.astype(np.uint8).reshape(k // 512, 16, n))


def unpack_weight(words, scales, fmt):
    g, _, n = scales.shape
    words = np.ascontiguousarray(words).reshape(g, 128, n, -1)
    if fmt == "e4m3":
        vals = words.view(ml_dtypes.float8_e4m3fn).astype(np.float64)
    else:
        nib = np.empty((g, 128, n, 4), np.uint8)
        nib[..., 0::2] = words & 0xF
        nib[..., 1::2] = words >> 4
        vals = E2M1[nib]
    vals = vals * np.repeat(np.exp2(scales.astype(np.float64) - 127.0), 8, axis=1)[..., None]
    return vals.transpose(0, 1, 3, 2).reshape(g * 512, n)


D, T, I, Q, E = 512, 1024, 512, 512, 256


def setup_inputs():
    n = np.random.standard_normal
    idx = np.stack([np.random.permutation(T)[:I] for _ in range(8)])
    idx2 = np.stack([np.random.permutation(T)[:I] for _ in range(8)])
    idx3 = np.stack([np.random.permutation(T)[:I] for _ in range(8)])
    idx4 = np.stack([np.random.permutation(T)[:I] for _ in range(8)])
    fd = mx_kscale(D)
    fq = mx_kscale(Q)
    keysp = pack_weight(n((D, T)) / fd[:, None], "e2m1")
    mixp = pack_weight(n((Q, E)) * 1.0 / np.sqrt(Q) / fq[:, None], "e4m3")
    return {
        "query": (n((D, Q)) * 1.0 / np.sqrt(D) * fd[:, None]).astype(np.float32),
        "keys_words": keysp[0],
        "keys_scales": keysp[1],
        "rowf": (np.random.uniform(0.5, 2.0, (Q, 1)) * fq[:, None]).astype(np.float32),
        "mix_words": mixp[0],
        "mix_scales": mixp[1],
        "offs": striped8(idx),
        "offs2": striped8(idx2),
        "offs3": striped8(idx3),
        "offs4": striped8(idx4),
    }


def reference(query, keys_words, keys_scales, rowf, mix_words, mix_scales, offs, offs2, offs3, offs4):
    idx = unstriped8(offs)
    idx2 = unstriped8(offs2)
    idx3 = unstriped8(offs3)
    idx4 = unstriped8(offs4)
    keysu = unpack_weight(keys_words, keys_scales, "e2m1")
    mixu = unpack_weight(mix_words, mix_scales, "e4m3")
    queryq = mxq(f64(query), 0, "e4m3")
    a = queryq.T @ keysu
    hi1 = np.maximum(pick8(a, idx, 64), pick8(a, idx2, 64))
    lo1 = np.minimum(pick8(a, idx, 64), pick8(a, idx2, 64))
    f1 = np.zeros((Q, T))
    f1[np.arange(Q)[:, None], idx3[np.arange(Q) % 512 // 64]] = hi1
    f2 = np.zeros((Q, T))
    f2[np.arange(Q)[:, None], idx4[np.arange(Q) % 512 // 64]] = lo1
    r = f1 - f2
    cc = a + r
    g = pick8(cc, idx, 64)
    gw = g * f64(rowf)
    gwq = mxq(gw, 0, "e4m3")
    y = mixu.T @ gwq
    return y

from contextlib import ExitStack

import concourse.mybir as mybir

D, T, I, Q, E = 512, 1024, 512, 512, 256
FLOPS = 2 * D * Q * T + 2 * Q * E * I

F32 = mybir.dt.float32
BF16 = mybir.dt.bfloat16
I32 = mybir.dt.int32
U32 = mybir.dt.uint32
U16 = mybir.dt.uint16
U8 = mybir.dt.uint8
FP8X4 = mybir.dt.float8_e4m3fn_x4
FP4X4 = mybir.dt.float4_e2m1fn_x4
ALU = mybir.AluOpType
COPY = mybir.ActivationFunctionType.Copy

P = 128
PACK = 4
BANK = 512
HALF = I // 2
LIST_COLS = I // 16


def load_scale_rows(queue, plane, rows):
    for quad in range(4):
        queue.dma_start(
            out=plane[32 * quad : 32 * quad + 4, :].bitcast(I32),
            in_=rows[4 * quad : 4 * quad + 4, :].bitcast(I32),
        )


def tile_attend_highlow_one_mixed_kernel(
    tc, query, keys_words, keys_scales, rowf, mix_words, mix_scales, offs, offs2, offs3, offs4, out
):
    nc = tc.nc
    with ExitStack() as ctx:
        sb = ctx.enter_context(tc.tile_pool(name="sb", bufs=1))
        ps = ctx.enter_context(tc.psum_pool(name="ps", bufs=1))

        def slot_half(offsets, h):
            return offsets[:, h * LIST_COLS // 2 : (h + 1) * LIST_COLS // 2]

        q_rows = query.rearrange("(p j) q -> p j q", j=PACK)
        raw = []
        for h in range(2):
            t = sb.tile([P, PACK, Q // 2], F32, name=f"raw{h}", tag=f"stage{h}", align_bytes=64)
            nc.sync.dma_start(out=t[:], in_=q_rows[:, :, h * Q // 2 : (h + 1) * Q // 2])
            raw.append(t)
        key_words = sb.tile([P, 2 * T], U8, name="key_words", align_bytes=64)
        nc.sync.dma_start(out=key_words[:].bitcast(I32), in_=keys_words[0].bitcast(I32))
        key_plane = sb.tile([P, T], U8, name="key_plane", align_bytes=64)
        nc.vector.memset(key_plane[:].bitcast(I32), 0)
        load_scale_rows(nc.scalar, key_plane, keys_scales[0])
        lists = []
        for n, src in enumerate((offs, offs2, offs3, offs4)):
            t = sb.tile([P, LIST_COLS], U16, name=f"list{n}")
            nc.sync.dma_start(t[:], src)
            lists.append(t)
        idx, idx2, idx3, idx4 = lists

        f1 = sb.tile([P, T], F32, name="f1")
        f2 = sb.tile([P, T], F32, name="f2")
        nc.vector.memset(f1[:], 0.0)
        nc.vector.memset(f2[:], 0.0)

        q_bf = sb.tile([P, PACK, P, PACK], BF16, name="q_bf", align_bytes=64)
        q_codes = sb.tile([P, Q], U32, name="q_codes", align_bytes=64)
        q_plane = sb.tile([P, Q], U8, name="q_plane", align_bytes=64)

        def deal(h, r0, r1):
            s_cols = slice(h * P // 2, (h + 1) * P // 2)
            nc.vector.tensor_copy(
                out=q_bf[:, r0:r1, s_cols, :].rearrange("p r s j -> p s j r"),
                in_=raw[h][:].rearrange("p j (s r) -> p s j r", r=PACK)[:, :, :, r0:r1],
            )

        def quantise_queries(r0, r1):
            nc.vector.quantize_mx(
                out=q_codes[:, r0 * P : r1 * P].bitcast(FP8X4),
                scales=q_plane[:, r0 * P : r1 * P],
                in_=q_bf[:, r0:r1, :, :].rearrange("p r s j -> p (r s j)"),
            )

        def score(r):
            banks = []
            for b in range(T // BANK):
                bank = ps.tile([P, BANK], F32, name=f"a_bank{r}{b}", tag=f"bank{2 * r + b}")
                nc.tensor.matmul_mx(
                    out=bank[:],
                    lhsT=q_codes[:, r * P : (r + 1) * P].bitcast(FP8X4),
                    lhsT_scale=q_plane[:, r * P : (r + 1) * P],
                    rhs=key_words[:, 2 * b * BANK : 2 * (b + 1) * BANK].bitcast(FP4X4),
                    rhs_scale=key_plane[:, b * BANK : (b + 1) * BANK],
                    start=True,
                    stop=True,
                )
                banks.append(bank)
            return banks

        deal(0, 0, PACK)
        deal(1, 0, 1)
        quantise_queries(0, 1)
        a_banks = [score(0)]
        deal(1, 1, PACK)
        quantise_queries(1, 2)
        quantise_queries(2, PACK)
        for r in range(1, PACK):
            a_banks.append(score(r))

        mix_codes = sb.tile([P, E], U32, name="mix_codes", tag="stage0", align_bytes=64)
        nc.sync.dma_start(
            out=mix_codes[:].bitcast(I32),
            in_=mix_words[0].rearrange("p n t -> p (n t)").bitcast(I32),
        )
        mix_plane = sb.tile([P, E], U8, name="mix_plane", tag="stage1", align_bytes=64)
        nc.gpsimd.memset(mix_plane[:].bitcast(I32), 0)
        load_scale_rows(nc.sync, mix_plane, mix_scales[0])
        row_factor = sb.tile([P, PACK], F32, name="row_factor")
        nc.gpsimd.dma_start(out=row_factor[:], in_=rowf.rearrange("(p r) o -> p (r o)", r=PACK))

        a = [sb.tile([P, T], F32, name=f"a{r}") for r in range(PACK)]
        cc = [sb.tile([P, T], F32, name=f"cc{r}") for r in range(PACK)]
        first = [sb.tile([P, I], F32, name=f"first{r}") for r in range(PACK)]
        second0 = sb.tile([P, I], F32, name="second0")
        hi0 = sb.tile([P, I], F32, name="hi0")
        second = [second0[:]] + [cc[r][:, :I] for r in range(PACK - 1)]
        hi = [hi0[:]] + [first[r][:] for r in range(PACK - 1)]
        lo = [first[r][:] for r in range(PACK)]

        halves = [slice(0, HALF), slice(HALF, I)]
        nc.scalar.copy(out=a[0][:, :BANK], in_=a_banks[0][0][:])
        nc.vector.tensor_copy(out=a[0][:, BANK:], in_=a_banks[0][1][:])
        nc.vector.tensor_copy(first[0][:, halves[0]], a[0][:].indirect(slot_half(idx, 0)))
        nc.scalar.activation(second[0][:, halves[0]], a[0][:].indirect(slot_half(idx2, 0)), COPY)
        nc.scalar.activation(first[0][:, halves[1]], a[0][:].indirect(slot_half(idx, 1)), COPY)
        nc.scalar.activation(second[0][:, halves[1]], a[0][:].indirect(slot_half(idx2, 1)), COPY)
        for r in range(1, PACK):
            for b in range(T // BANK):
                nc.scalar.copy(out=a[r][:, b * BANK : (b + 1) * BANK], in_=a_banks[r][b][:])
            nc.scalar.activation(first[r][:], a[r][:].indirect(idx[:]), COPY)
            nc.scalar.activation(second[r], a[r][:].indirect(idx2[:]), COPY)

        part = sb.tile([P, T], F32, name="part")
        g = sb.tile([P, I], F32, name="g")
        gw_bf = sb.tile([P, I, PACK], BF16, name="gw_bf", align_bytes=64)

        def finish(r):
            nc.gpsimd.tensor_tensor(cc[r][:], part[:], f2[:], ALU.subtract)
            nc.scalar.activation(g[:], cc[r][:].indirect(idx[:]), COPY)
            nc.scalar.activation(gw_bf[:, :, r], g[:], COPY, scale=row_factor[:, r : r + 1])

        for r in range(PACK):
            if r == 0:
                for h in range(2):
                    nc.vector.tensor_tensor(hi[0][:, halves[h]], first[0][:, halves[h]], second[0][:, halves[h]], ALU.max)
                    if h == 1:
                        nc.vector.tensor_tensor(lo[0], first[0][:], second[0], ALU.min)
                    nc.vector.tensor_copy(f1[:].indirect(slot_half(idx3, h)), hi[0][:, halves[h]])
            else:
                nc.vector.tensor_tensor(hi[r], first[r][:], second[r], ALU.max)
                nc.vector.tensor_tensor(lo[r], first[r][:], second[r], ALU.min)
                nc.vector.tensor_copy(f1[:].indirect(idx3[:]), hi[r])
                finish(r - 1)
            nc.vector.tensor_copy(f2[:].indirect(idx4[:]), lo[r])
            nc.gpsimd.tensor_tensor(part[:], a[r][:], f1[:], ALU.add)

        last = PACK - 1
        gw_codes = sb.tile([P, I], U32, name="gw_codes", align_bytes=64)
        gw_plane = sb.tile([P, I], U8, name="gw_plane", align_bytes=64)
        nc.vector.tensor_tensor(cc[last][:], part[:], f2[:], ALU.subtract)
        nc.vector.tensor_copy(g[:, halves[0]], cc[last][:].indirect(slot_half(idx, 0)))
        nc.scalar.activation(g[:, halves[1]], cc[last][:].indirect(slot_half(idx, 1)), COPY)
        for h in range(2):
            nc.vector.tensor_scalar(
                gw_bf[:, halves[h], last], g[:, halves[h]], row_factor[:, last : last + 1], None, ALU.mult
            )
        for h in range(2):
            nc.vector.quantize_mx(
                out=gw_codes[:, halves[h]].bitcast(FP8X4),
                scales=gw_plane[:, halves[h]],
                in_=gw_bf[:, halves[h], :].rearrange("p i r -> p (i r)"),
            )
        for h in range(2):
            for c in range(E // P):
                bank = ps.tile([P, HALF], F32, name=f"y_bank{h}{c}", tag=f"bank{2 * h + c}")
                nc.tensor.matmul_mx(
                    out=bank[:],
                    lhsT=mix_codes[:, c * P : (c + 1) * P].bitcast(FP8X4),
                    lhsT_scale=mix_plane[:, c * P : (c + 1) * P],
                    rhs=gw_codes[:, halves[h]].bitcast(FP8X4),
                    rhs_scale=gw_plane[:, halves[h]],
                    start=True,
                    stop=True,
                )
                y = sb.tile([P, HALF], F32, name=f"y{h}{c}")
                if h == 1 and c == 1:
                    nc.vector.tensor_copy(out=y[:], in_=bank[:])
                else:
                    nc.scalar.copy(out=y[:], in_=bank[:])
                nc.sync.dma_start(out=out[c * P : (c + 1) * P, halves[h]], in_=y[:])
